import numpy as np
import ml_dtypes


def mxq(x, axis, fmt="e4m3"):
    dtype, down = {"e4m3": (ml_dtypes.float8_e4m3fn, 7), "e5m2": (ml_dtypes.float8_e5m2, 14)}[fmt]
    v = np.moveaxis(np.asarray(x, np.float32).astype(ml_dtypes.bfloat16).astype(np.float64), axis, -1)
    blocks = v.reshape(v.shape[:-1] + (-1, 32))
    amax = np.abs(blocks).max(-1, keepdims=True)
    byte = np.maximum(np.where(amax > 0, np.frexp(amax)[1] - 1 + 127, 0) - down, 1)
    scale = np.exp2(byte - 127.0)
    codes = (blocks / scale).astype(np.float32).astype(dtype).astype(np.float64)
    return np.moveaxis((codes * scale).reshape(v.shape), -1, axis)


WIDE = False


def mx_kscale(k):
    if not WIDE:
        return np.ones(k)
    levels = np.array([10, -10, 5, -5, 0])
    if k % 512:
        return np.exp2(np.random.permutation(np.resize(levels, k // 32))).repeat(32)
    a = np.empty((k // 512, 16))
    for p in range(k // 512):
        a[p, :8] = np.random.permutation(np.resize(levels, 8))
        for g in range(8):
            far = levels[np.abs(levels - a[p, g]) >= 10]
            a[p, g + 8] = far[np.random.randint(len(far))]
    return np.exp2(a.ravel()).repeat(32)


def f64(x):
    return np.asarray(x).astype(np.float64)


def striped(idx):
    return np.tile(idx.reshape(-1, 16).T, (8, 1)).astype(np.uint16)


def unstriped(offs):
    return offs[:16].T.reshape(-1).astype(np.int64)


K, T, E, C, N = 2048, 1024, 2, 256, 256


def by_expert(wq, xq):
    return np.concatenate([wq[e].T @ xq[:, e * C:(e + 1) * C] for e in range(E)], axis=1)


def setup_inputs():
    n = np.random.standard_normal
    s = mx_kscale(K)[:, None]
    return {
        "xT": (n((K, T)) * s).astype(np.float32),
        "w": (n((E, K, N)) / np.sqrt(K) / s[None]).astype(np.float32),
        "offs": striped(np.random.permutation(T)[:E * C]),
    }


def reference(xT, w, offs):
    idx = unstriped(offs)
    xq = mxq(f64(xT)[:, idx], 0, "e4m3")
    y = by_expert(mxq(f64(w), 1, "e4m3"), xq)
    out = np.zeros((N, T))
    out[:, idx] = y
    return out

@@ -1,0 +1,103 @@
+from contextlib import ExitStack
+
+import concourse.mybir as mybir
+
+K, T, E, C, N = 2048, 1024, 2, 256, 256
+FLOPS = 2 * K * E * C * N
+
+F32 = mybir.dt.float32
+BF16 = mybir.dt.bfloat16
+U32 = mybir.dt.uint32
+U16 = mybir.dt.uint16
+U8 = mybir.dt.uint8
+FP8X4 = mybir.dt.float8_e4m3fn_x4
+
+P = 128
+PASSES = K // 512
+SLOTS = E * C
+XG = 256
+WG = 96
+MULT = mybir.AluOpType.mult
+ADD = mybir.AluOpType.add
+
+
+def tile_routed_moe_kernel(tc, xT, w, offs, out):
+    nc = tc.nc
+    with ExitStack() as ctx:
+        lists = ctx.enter_context(tc.tile_pool(name="lists", bufs=1))
+        keep = ctx.enter_context(tc.tile_pool(name="keep", bufs=1))
+        psum = ctx.enter_context(tc.psum_pool(name="psum", bufs=1))
+
+        offsets = lists.tile([P, SLOTS // 16], U16, name="offsets")
+        nc.sync.dma_start(offsets[:], offs)
+
+        xv = xT.rearrange("(g p t) n -> g p t n", p=P, t=4)
+        wv = w.rearrange("e (g p j) n -> e g p j n", p=P, j=4)
+
+        xraw = {}
+        for g in range(PASSES):
+            for u in range(2):
+                xraw[g, u] = keep.tile([P, 2, T], F32, name="xraw%d%d" % (g, u))
+                nc.sync.dma_start(out=xraw[g, u][:], in_=xv[g, :, 2 * u : 2 * u + 2, :])
+        wraw = {}
+        for e in range(E):
+            for g in range(PASSES):
+                wraw[e, g] = keep.tile([P, 4, N], F32, name="wraw%d%d" % (e, g))
+                nc.sync.dma_start(out=wraw[e, g][:], in_=wv[e, g])
+
+        window = []
+        for m in range(N // P):
+            window.append(keep.tile([P, T], F32, name="window%d" % m))
+            nc.vector.memset(window[m][:], 0.0)
+
+        xcodes, xscales = {}, {}
+        for g in range(PASSES):
+            xg = keep.tile([P, SLOTS * 4], BF16, name="xg%d" % g, align_bytes=64)
+            xg_words = xg[:].bitcast(U32).rearrange("p (c u) -> p c u", u=2)
+            for u in range(2):
+                pair = keep.tile([P, T, 2], BF16, name="pair%d%d" % (g, u))
+                src = xraw[g, u][:].rearrange("p e n -> p n e")
+                nc.scalar.copy(out=pair[:, XG:, :], in_=src[:, XG:, :])
+                nc.gpsimd.tensor_scalar(pair[:, :XG, :], src[:, :XG, :], 1.0, 0.0, MULT, ADD)
+                words = pair[:].rearrange("p n e -> p (n e)").bitcast(U32)
+                nc.vector.tensor_copy(out=xg_words[:, :, u], in_=words.indirect(offsets[:]))
+            xcodes[g] = keep.tile([P, SLOTS], U32, name="xcodes%d" % g, align_bytes=64)
+            xscales[g] = keep.tile([P, SLOTS], U8, name="xscales%d" % g, align_bytes=64)
+            nc.vector.quantize_mx(out=xcodes[g][:].bitcast(FP8X4), scales=xscales[g][:], in_=xg[:])
+
+        for e in range(E):
+            acc = [psum.tile([P, C], F32, name="acc%d%d" % (e, m)) for m in range(N // P)]
+            for g in range(PASSES):
+                wb = keep.tile([P, N, 4], BF16, name="wb%d%d" % (e, g), align_bytes=64)
+                src = wraw[e, g][:].rearrange("p j n -> p n j")
+                nc.scalar.copy(out=wb[:, WG:, :], in_=src[:, WG:, :])
+                nc.gpsimd.tensor_scalar(wb[:, :WG, :], src[:, :WG, :], 1.0, 0.0, MULT, ADD)
+                wcodes = keep.tile([P, N], U32, name="wcodes%d%d" % (e, g), align_bytes=64)
+                wscales = keep.tile([P, N], U8, name="wscales%d%d" % (e, g), align_bytes=64)
+                nc.vector.quantize_mx(
+                    out=wcodes[:].bitcast(FP8X4),
+                    scales=wscales[:],
+                    in_=wb[:].rearrange("p n j -> p (n j)"),
+                )
+                for m in range(N // P):
+                    nc.tensor.matmul_mx(
+                        out=acc[m][:],
+                        lhsT=wcodes[:, m * P : (m + 1) * P].bitcast(FP8X4),
+                        lhsT_scale=wscales[:, m * P : (m + 1) * P],
+                        rhs=xcodes[g][:, e * C : (e + 1) * C].bitcast(FP8X4),
+                        rhs_scale=xscales[g][:, e * C : (e + 1) * C],
+                        start=(g == 0),
+                        stop=(g == PASSES - 1),
+                    )
+            for m in range(N // P):
+                y = keep.tile([P, C], F32, name="y%d%d" % (e, m))
+                if m == 0:
+                    nc.vector.tensor_copy(out=y[:], in_=acc[m][:])
+                else:
+                    nc.scalar.copy(out=y[:], in_=acc[m][:])
+                nc.vector.tensor_copy(
+                    out=window[m][:].indirect(offsets[:, e * (C // 16) : (e + 1) * (C // 16)]),
+                    in_=y[:],
+                )
+                if e == E - 1:
+                    nc.sync.dma_start(out=out[m * P : (m + 1) * P, :], in_=window[m][:])

@@ -15,10 +15,11 @@ FP8X4 = mybir.dt.float8_e4m3fn_x4
 P = 128
 PASSES = K // 512
 SLOTS = E * C
-XG = 256
-WG = 96
+MT = N // P
 MULT = mybir.AluOpType.mult
 ADD = mybir.AluOpType.add
+XG = 256
+WG = 96
 
 
 def tile_routed_moe_kernel(tc, xT, w, offs, out):
@@ -46,7 +47,7 @@ def tile_routed_moe_kernel(tc, xT, w, offs, out):
                 nc.sync.dma_start(out=wraw[e, g][:], in_=wv[e, g])
 
         window = []
-        for m in range(N // P):
+        for m in range(MT):
             window.append(keep.tile([P, T], F32, name="window%d" % m))
             nc.vector.memset(window[m][:], 0.0)
 
@@ -65,39 +66,51 @@ def tile_routed_moe_kernel(tc, xT, w, offs, out):
             xscales[g] = keep.tile([P, SLOTS], U8, name="xscales%d" % g, align_bytes=64)
             nc.vector.quantize_mx(out=xcodes[g][:].bitcast(FP8X4), scales=xscales[g][:], in_=xg[:])
 
+        acc = {}
         for e in range(E):
-            acc = [psum.tile([P, C], F32, name="acc%d%d" % (e, m)) for m in range(N // P)]
-            for g in range(PASSES):
-                wb = keep.tile([P, N, 4], BF16, name="wb%d%d" % (e, g), align_bytes=64)
-                src = wraw[e, g][:].rearrange("p j n -> p n j")
-                nc.scalar.copy(out=wb[:, WG:, :], in_=src[:, WG:, :])
-                nc.gpsimd.tensor_scalar(wb[:, :WG, :], src[:, :WG, :], 1.0, 0.0, MULT, ADD)
-                wcodes = keep.tile([P, N], U32, name="wcodes%d%d" % (e, g), align_bytes=64)
-                wscales = keep.tile([P, N], U8, name="wscales%d%d" % (e, g), align_bytes=64)
-                nc.vector.quantize_mx(
-                    out=wcodes[:].bitcast(FP8X4),
-                    scales=wscales[:],
-                    in_=wb[:].rearrange("p n j -> p (n j)"),
+            for m in range(MT):
+                acc[e, m] = psum.tile([P, C], F32, name="acc%d%d" % (e, m))
+
+        def multiply(e, g, name):
+            wb = keep.tile([P, N, 4], BF16, name=name, align_bytes=64)
+            src = wraw[e, g][:].rearrange("p j n -> p n j")
+            nc.scalar.copy(out=wb[:, WG:, :], in_=src[:, WG:, :])
+            nc.gpsimd.tensor_scalar(wb[:, :WG, :], src[:, :WG, :], 1.0, 0.0, MULT, ADD)
+            wcodes = keep.tile([P, N], U32, name="wcodes%d%d" % (e, g), align_bytes=64)
+            wscales = keep.tile([P, N], U8, name="wscales%d%d" % (e, g), align_bytes=64)
+            nc.vector.quantize_mx(
+                out=wcodes[:].bitcast(FP8X4),
+                scales=wscales[:],
+                in_=wb[:].rearrange("p n j -> p (n j)"),
+            )
+            for m in range(MT):
+                nc.tensor.matmul_mx(
+                    out=acc[e, m][:],
+                    lhsT=wcodes[:, m * P : (m + 1) * P].bitcast(FP8X4),
+                    lhsT_scale=wscales[:, m * P : (m + 1) * P],
+                    rhs=xcodes[g][:, e * C : (e + 1) * C].bitcast(FP8X4),
+                    rhs_scale=xscales[g][:, e * C : (e + 1) * C],
+                    start=(g == 0),
+                    stop=(g == PASSES - 1),
                 )
-                for m in range(N // P):
-                    nc.tensor.matmul_mx(
-                        out=acc[m][:],
-                        lhsT=wcodes[:, m * P : (m + 1) * P].bitcast(FP8X4),
-                        lhsT_scale=wscales[:, m * P : (m + 1) * P],
-                        rhs=xcodes[g][:, e * C : (e + 1) * C].bitcast(FP8X4),
-                        rhs_scale=xscales[g][:, e * C : (e + 1) * C],
-                        start=(g == 0),
-                        stop=(g == PASSES - 1),
-                    )
-            for m in range(N // P):
-                y = keep.tile([P, C], F32, name="y%d%d" % (e, m))
-                if m == 0:
-                    nc.vector.tensor_copy(out=y[:], in_=acc[m][:])
-                else:
-                    nc.scalar.copy(out=y[:], in_=acc[m][:])
-                nc.vector.tensor_copy(
-                    out=window[m][:].indirect(offsets[:, e * (C // 16) : (e + 1) * (C // 16)]),
-                    in_=y[:],
-                )
-                if e == E - 1:
-                    nc.sync.dma_start(out=out[m * P : (m + 1) * P, :], in_=window[m][:])
+
+        def put_back(e, m, name):
+            y = keep.tile([P, C], F32, name=name, align_bytes=64)
+            nc.scalar.copy(out=y[:], in_=acc[e, m][:])
+            nc.vector.tensor_copy(
+                out=window[m][:].indirect(offsets[:, e * (C // 16) : (e + 1) * (C // 16)]),
+                in_=y[:],
+            )
+            if e == E - 1:
+                nc.sync.dma_start(out=out[m * P : (m + 1) * P, :], in_=window[m][:])
+
+        for g in range(PASSES):
+            multiply(0, g, "wb0%d" % g)
+        put_back(0, 0, "y00")
+        for g in range(2 + 1):
+            multiply(1, g, "shared" if g == 2 else "wb1%d" % g)
+        put_back(0, 1, "shared")
+        for g in range(2 + 1, PASSES):
+            multiply(1, g, "wb1%d" % g)
+        put_back(1, 0, "y10")
+        put_back(1, 1, "y11")

@@ -74,7 +74,10 @@ def tile_routed_moe_kernel(tc, xT, w, offs, out):
         def multiply(e, g, name):
             wb = keep.tile([P, N, 4], BF16, name=name, align_bytes=64)
             src = wraw[e, g][:].rearrange("p j n -> p n j")
-            nc.scalar.copy(out=wb[:, WG:, :], in_=src[:, WG:, :])
+            nc.scalar.copy(
+                out=wb[:, WG:, :].rearrange("p (c i) j -> p c j i", i=4),
+                in_=wraw[e, g][:, :, WG:].rearrange("p j (c i) -> p c j i", i=4),
+            )
             nc.gpsimd.tensor_scalar(wb[:, :WG, :], src[:, :WG, :], 1.0, 0.0, MULT, ADD)
             wcodes = keep.tile([P, N], U32, name="wcodes%d%d" % (e, g), align_bytes=64)
             wscales = keep.tile([P, N], U8, name="wscales%d%d" % (e, g), align_bytes=64)

@@ -18,8 +18,8 @@ SLOTS = E * C
 MT = N // P
 MULT = mybir.AluOpType.mult
 ADD = mybir.AluOpType.add
+XG_LAST = 512
 XG = 256
-WG = 96
 
 
 def tile_routed_moe_kernel(tc, xT, w, offs, out):
@@ -43,7 +43,8 @@ def tile_routed_moe_kernel(tc, xT, w, offs, out):
         wraw = {}
         for e in range(E):
             for g in range(PASSES):
-                wraw[e, g] = keep.tile([P, 4, N], F32, name="wraw%d%d" % (e, g))
+                name = "shared" if (e, g) == (E - 1, PASSES - 1) else "wraw%d%d" % (e, g)
+                wraw[e, g] = keep.tile([P, 4, N], F32, name=name, align_bytes=64)
                 nc.sync.dma_start(out=wraw[e, g][:], in_=wv[e, g])
 
         window = []
@@ -58,8 +59,9 @@ def tile_routed_moe_kernel(tc, xT, w, offs, out):
             for u in range(2):
                 pair = keep.tile([P, T, 2], BF16, name="pair%d%d" % (g, u))
                 src = xraw[g, u][:].rearrange("p e n -> p n e")
-                nc.scalar.copy(out=pair[:, XG:, :], in_=src[:, XG:, :])
-                nc.gpsimd.tensor_scalar(pair[:, :XG, :], src[:, :XG, :], 1.0, 0.0, MULT, ADD)
+                cut = XG_LAST if (g, u) == (PASSES - 1, 1) else XG
+                nc.scalar.copy(out=pair[:, cut:, :], in_=src[:, cut:, :])
+                nc.gpsimd.tensor_scalar(pair[:, :cut, :], src[:, :cut, :], 1.0, 0.0, MULT, ADD)
                 words = pair[:].rearrange("p n e -> p (n e)").bitcast(U32)
                 nc.vector.tensor_copy(out=xg_words[:, :, u], in_=words.indirect(offsets[:]))
             xcodes[g] = keep.tile([P, SLOTS], U32, name="xcodes%d" % g, align_bytes=64)
@@ -73,12 +75,10 @@ def tile_routed_moe_kernel(tc, xT, w, offs, out):
 
         def multiply(e, g, name):
             wb = keep.tile([P, N, 4], BF16, name=name, align_bytes=64)
-            src = wraw[e, g][:].rearrange("p j n -> p n j")
             nc.scalar.copy(
-                out=wb[:, WG:, :].rearrange("p (c i) j -> p c j i", i=4),
-                in_=wraw[e, g][:, :, WG:].rearrange("p j (c i) -> p c j i", i=4),
+                out=wb[:].rearrange("p (c i) j -> p c j i", i=4),
+                in_=wraw[e, g][:].rearrange("p j (c i) -> p c j i", i=4),
             )
-            nc.gpsimd.tensor_scalar(wb[:, :WG, :], src[:, :WG, :], 1.0, 0.0, MULT, ADD)
             wcodes = keep.tile([P, N], U32, name="wcodes%d%d" % (e, g), align_bytes=64)
             wscales = keep.tile([P, N], U8, name="wscales%d%d" % (e, g), align_bytes=64)
             nc.vector.quantize_mx(
@@ -99,7 +99,10 @@ def tile_routed_moe_kernel(tc, xT, w, offs, out):
 
         def put_back(e, m, name):
             y = keep.tile([P, C], F32, name=name, align_bytes=64)
-            nc.scalar.copy(out=y[:], in_=acc[e, m][:])
+            if (e, m) == (0, 0):
+                nc.vector.tensor_copy(out=y[:], in_=acc[e, m][:])
+            else:
+                nc.scalar.copy(out=y[:], in_=acc[e, m][:])
             nc.vector.tensor_copy(
                 out=window[m][:].indirect(offsets[:, e * (C // 16) : (e + 1) * (C // 16)]),
                 in_=y[:],
@@ -110,10 +113,8 @@ def tile_routed_moe_kernel(tc, xT, w, offs, out):
         for g in range(PASSES):
             multiply(0, g, "wb0%d" % g)
         put_back(0, 0, "y00")
-        for g in range(2 + 1):
-            multiply(1, g, "shared" if g == 2 else "wb1%d" % g)
-        put_back(0, 1, "shared")
-        for g in range(2 + 1, PASSES):
+        for g in range(PASSES):
             multiply(1, g, "wb1%d" % g)
+        put_back(0, 1, "shared")
         put_back(1, 0, "y10")
         put_back(1, 1, "y11")

@@ -18,8 +18,11 @@ SLOTS = E * C
 MT = N // P
 MULT = mybir.AluOpType.mult
 ADD = mybir.AluOpType.add
-XG_LAST = 512
 XG = 256
+XG_LAST = 512
+WG = {(1, 2): 64, (0, 0): 64, (0, 1): 64}
+BY_TILE = [(0, 3), (1, 3)]
+SPLIT_LOADS = [(1, 3)]
 
 
 def tile_routed_moe_kernel(tc, xT, w, offs, out):
@@ -43,9 +46,13 @@ def tile_routed_moe_kernel(tc, xT, w, offs, out):
         wraw = {}
         for e in range(E):
             for g in range(PASSES):
-                name = "shared" if (e, g) == (E - 1, PASSES - 1) else "wraw%d%d" % (e, g)
-                wraw[e, g] = keep.tile([P, 4, N], F32, name=name, align_bytes=64)
-                nc.sync.dma_start(out=wraw[e, g][:], in_=wv[e, g])
+                parts = MT if (e, g) in SPLIT_LOADS else 1
+                width = N // parts
+                for i in range(parts):
+                    raw = keep.tile([P, 4, width], F32, name="wraw%d%d%d" % (e, g, i), align_bytes=64)
+                    nc.sync.dma_start(out=raw[:], in_=wv[e, g, :, :, i * width : (i + 1) * width])
+                    for m in range(i * MT // parts, (i + 1) * MT // parts):
+                        wraw[e, g, m] = (raw, i * width)
 
         window = []
         for m in range(MT):
@@ -68,41 +75,52 @@ def tile_routed_moe_kernel(tc, xT, w, offs, out):
             xscales[g] = keep.tile([P, SLOTS], U8, name="xscales%d" % g, align_bytes=64)
             nc.vector.quantize_mx(out=xcodes[g][:].bitcast(FP8X4), scales=xscales[g][:], in_=xg[:])
 
-        acc = {}
-        for e in range(E):
-            for m in range(MT):
-                acc[e, m] = psum.tile([P, C], F32, name="acc%d%d" % (e, m))
+        weights = {}
 
-        def multiply(e, g, name):
+        def prepare(e, g, name):
             wb = keep.tile([P, N, 4], BF16, name=name, align_bytes=64)
-            nc.scalar.copy(
-                out=wb[:].rearrange("p (c i) j -> p c j i", i=4),
-                in_=wraw[e, g][:].rearrange("p j (c i) -> p c j i", i=4),
-            )
-            wcodes = keep.tile([P, N], U32, name="wcodes%d%d" % (e, g), align_bytes=64)
-            wscales = keep.tile([P, N], U8, name="wscales%d%d" % (e, g), align_bytes=64)
-            nc.vector.quantize_mx(
-                out=wcodes[:].bitcast(FP8X4),
-                scales=wscales[:],
-                in_=wb[:].rearrange("p n j -> p (n j)"),
-            )
-            for m in range(MT):
+            parts = MT if (e, g) in BY_TILE else 1
+            width = N // parts
+            for i in range(parts):
+                lo, hi = i * width, (i + 1) * width
+                raw, base = wraw[e, g, lo // P]
+                mid = lo + WG.get((e, g), 0) // parts
+                nc.scalar.copy(
+                    out=wb[:, mid:hi, :].rearrange("p (c i) j -> p c j i", i=4),
+                    in_=raw[:, :, mid - base : hi - base].rearrange("p j (c i) -> p c j i", i=4),
+                )
+                if mid > lo:
+                    src = raw[:, :, lo - base : mid - base].rearrange("p j n -> p n j")
+                    nc.gpsimd.tensor_scalar(wb[:, lo:mid, :], src, 1.0, 0.0, MULT, ADD)
+                codes = keep.tile([P, width], U32, name="wcodes%d%d%d" % (e, g, i), align_bytes=64)
+                scales = keep.tile([P, width], U8, name="wscales%d%d%d" % (e, g, i), align_bytes=64)
+                nc.vector.quantize_mx(
+                    out=codes[:].bitcast(FP8X4),
+                    scales=scales[:],
+                    in_=wb[:, lo:hi, :].rearrange("p n j -> p (n j)"),
+                )
+                for m in range(lo // P, hi // P):
+                    cols = slice(m * P - lo, (m + 1) * P - lo)
+                    weights[e, g, m] = (codes[:, cols].bitcast(FP8X4), scales[:, cols])
+
+        def put_back(e, m, name):
+            acc = psum.tile([P, C], F32, name="acc0" if e == 0 else "acc1%d" % m)
+            for g in range(PASSES):
+                codes, scales = weights[e, g, m]
                 nc.tensor.matmul_mx(
-                    out=acc[e, m][:],
-                    lhsT=wcodes[:, m * P : (m + 1) * P].bitcast(FP8X4),
-                    lhsT_scale=wscales[:, m * P : (m + 1) * P],
+                    out=acc[:],
+                    lhsT=codes,
+                    lhsT_scale=scales,
                     rhs=xcodes[g][:, e * C : (e + 1) * C].bitcast(FP8X4),
                     rhs_scale=xscales[g][:, e * C : (e + 1) * C],
                     start=(g == 0),
                     stop=(g == PASSES - 1),
                 )
-
-        def put_back(e, m, name):
             y = keep.tile([P, C], F32, name=name, align_bytes=64)
             if (e, m) == (0, 0):
-                nc.vector.tensor_copy(out=y[:], in_=acc[e, m][:])
+                nc.vector.tensor_copy(out=y[:], in_=acc[:])
             else:
-                nc.scalar.copy(out=y[:], in_=acc[e, m][:])
+                nc.scalar.copy(out=y[:], in_=acc[:])
             nc.vector.tensor_copy(
                 out=window[m][:].indirect(offsets[:, e * (C // 16) : (e + 1) * (C // 16)]),
                 in_=y[:],
@@ -111,10 +129,10 @@ def tile_routed_moe_kernel(tc, xT, w, offs, out):
                 nc.sync.dma_start(out=out[m * P : (m + 1) * P, :], in_=window[m][:])
 
         for g in range(PASSES):
-            multiply(0, g, "wb0%d" % g)
+            prepare(0, g, "wb0%d" % g)
         put_back(0, 0, "y00")
         for g in range(PASSES):
-            multiply(1, g, "wb1%d" % g)
-        put_back(0, 1, "shared")
+            prepare(1, g, "wb1%d" % g)
+        put_back(0, 1, "wraw130")
         put_back(1, 0, "y10")
         put_back(1, 1, "y11")

@@ -20,7 +20,7 @@ MULT = mybir.AluOpType.mult
 ADD = mybir.AluOpType.add
 XG = 256
 XG_LAST = 512
-WG = {(1, 2): 64, (0, 0): 64, (0, 1): 64}
+WG = {(1, 0): 96, (1, 1): 96, (1, 2): 96}
 BY_TILE = [(0, 3), (1, 3)]
 SPLIT_LOADS = [(1, 3)]
 
@@ -117,10 +117,7 @@ def tile_routed_moe_kernel(tc, xT, w, offs, out):
                     stop=(g == PASSES - 1),
                 )
             y = keep.tile([P, C], F32, name=name, align_bytes=64)
-            if (e, m) == (0, 0):
-                nc.vector.tensor_copy(out=y[:], in_=acc[:])
-            else:
-                nc.scalar.copy(out=y[:], in_=acc[:])
+            nc.scalar.copy(out=y[:], in_=acc[:])
             nc.vector.tensor_copy(
                 out=window[m][:].indirect(offsets[:, e * (C // 16) : (e + 1) * (C // 16)]),
                 in_=y[:],
@@ -133,6 +130,6 @@ def tile_routed_moe_kernel(tc, xT, w, offs, out):
         put_back(0, 0, "y00")
         for g in range(PASSES):
             prepare(1, g, "wb1%d" % g)
-        put_back(0, 1, "wraw130")
+        put_back(0, 1, "wraw120")
         put_back(1, 0, "y10")
         put_back(1, 1, "y11")

@@ -35,24 +35,29 @@ def tile_routed_moe_kernel(tc, xT, w, offs, out):
         offsets = lists.tile([P, SLOTS // 16], U16, name="offsets")
         nc.sync.dma_start(offsets[:], offs)
 
-        xv = xT.rearrange("(g p t) n -> g p t n", p=P, t=4)
-        wv = w.rearrange("e (g p j) n -> e g p j n", p=P, j=4)
+        xv = xT.rearrange("(g p u e) n -> g u p (e n)", p=P, u=2, e=2)
+        wv = w.rearrange("e (g p j) n -> e g p (j n)", p=P, j=4)
+        wv_tiles = w.rearrange("e (g p j) n -> e g p j n", p=P, j=4)
 
         xraw = {}
         for g in range(PASSES):
             for u in range(2):
-                xraw[g, u] = keep.tile([P, 2, T], F32, name="xraw%d%d" % (g, u))
-                nc.sync.dma_start(out=xraw[g, u][:], in_=xv[g, :, 2 * u : 2 * u + 2, :])
+                xraw[g, u] = keep.tile([P, 2 * T], F32, name="xraw%d%d" % (g, u))
+                nc.sync.dma_start(out=xraw[g, u][:], in_=xv[g, u])
         wraw = {}
         for e in range(E):
             for g in range(PASSES):
                 parts = MT if (e, g) in SPLIT_LOADS else 1
                 width = N // parts
                 for i in range(parts):
-                    raw = keep.tile([P, 4, width], F32, name="wraw%d%d%d" % (e, g, i), align_bytes=64)
-                    nc.sync.dma_start(out=raw[:], in_=wv[e, g, :, :, i * width : (i + 1) * width])
+                    raw = keep.tile([P, 4 * width], F32, name="wraw%d%d%d" % (e, g, i), align_bytes=64)
+                    rows = raw[:].rearrange("p (j n) -> p j n", j=4)
+                    if parts == 1:
+                        nc.sync.dma_start(out=raw[:], in_=wv[e, g])
+                    else:
+                        nc.sync.dma_start(out=rows, in_=wv_tiles[e, g, :, :, i * width : (i + 1) * width])
                     for m in range(i * MT // parts, (i + 1) * MT // parts):
-                        wraw[e, g, m] = (raw, i * width)
+                        wraw[e, g, m] = (rows, i * width)
 
         window = []
         for m in range(MT):
@@ -65,7 +70,7 @@ def tile_routed_moe_kernel(tc, xT, w, offs, out):
             xg_words = xg[:].bitcast(U32).rearrange("p (c u) -> p c u", u=2)
             for u in range(2):
                 pair = keep.tile([P, T, 2], BF16, name="pair%d%d" % (g, u))
-                src = xraw[g, u][:].rearrange("p e n -> p n e")
+                src = xraw[g, u][:].rearrange("p (e n) -> p n e", e=2)
                 cut = XG_LAST if (g, u) == (PASSES - 1, 1) else XG
                 nc.scalar.copy(out=pair[:, cut:, :], in_=src[:, cut:, :])
                 nc.gpsimd.tensor_scalar(pair[:, :cut, :], src[:, :cut, :], 1.0, 0.0, MULT, ADD)

from contextlib import ExitStack

import concourse.mybir as mybir

K, T, E, C, N = 2048, 1024, 2, 256, 256
FLOPS = 2 * K * E * C * N

F32 = mybir.dt.float32
BF16 = mybir.dt.bfloat16
U32 = mybir.dt.uint32
U16 = mybir.dt.uint16
U8 = mybir.dt.uint8
FP8X4 = mybir.dt.float8_e4m3fn_x4

P = 128
PASSES = K // 512
SLOTS = E * C
MT = N // P
MULT = mybir.AluOpType.mult
ADD = mybir.AluOpType.add
XG = 256
XG_LAST = 512
WG = {(1, 0): 96, (1, 1): 96, (1, 2): 96}
BY_TILE = [(0, 3), (1, 3)]
SPLIT_LOADS = [(1, 3)]


def tile_routed_moe_kernel(tc, xT, w, offs, out):
    nc = tc.nc
    with ExitStack() as ctx:
        lists = ctx.enter_context(tc.tile_pool(name="lists", bufs=1))
        keep = ctx.enter_context(tc.tile_pool(name="keep", bufs=1))
        psum = ctx.enter_context(tc.psum_pool(name="psum", bufs=1))

        offsets = lists.tile([P, SLOTS // 16], U16, name="offsets")
        nc.sync.dma_start(offsets[:], offs)

        xv = xT.rearrange("(g p u e) n -> g u p (e n)", p=P, u=2, e=2)
        wv = w.rearrange("e (g p j) n -> e g p (j n)", p=P, j=4)
        wv_tiles = w.rearrange("e (g p j) n -> e g p j n", p=P, j=4)

        xraw = {}
        for g in range(PASSES):
            for u in range(2):
                xraw[g, u] = keep.tile([P, 2 * T], F32, name="xraw%d%d" % (g, u))
                nc.sync.dma_start(out=xraw[g, u][:], in_=xv[g, u])
        wraw = {}
        for e in range(E):
            for g in range(PASSES):
                parts = MT if (e, g) in SPLIT_LOADS else 1
                width = N // parts
                for i in range(parts):
                    raw = keep.tile([P, 4 * width], F32, name="wraw%d%d%d" % (e, g, i), align_bytes=64)
                    rows = raw[:].rearrange("p (j n) -> p j n", j=4)
                    if parts == 1:
                        nc.sync.dma_start(out=raw[:], in_=wv[e, g])
                    else:
                        nc.sync.dma_start(out=rows, in_=wv_tiles[e, g, :, :, i * width : (i + 1) * width])
                    for m in range(i * MT // parts, (i + 1) * MT // parts):
                        wraw[e, g, m] = (rows, i * width)

        window = []
        for m in range(MT):
            window.append(keep.tile([P, T], F32, name="window%d" % m))
            nc.vector.memset(window[m][:], 0.0)

        xcodes, xscales = {}, {}
        for g in range(PASSES):
            xg = keep.tile([P, SLOTS * 4], BF16, name="xg%d" % g, align_bytes=64)
            xg_words = xg[:].bitcast(U32).rearrange("p (c u) -> p c u", u=2)
            for u in range(2):
                pair = keep.tile([P, T, 2], BF16, name="pair%d%d" % (g, u))
                src = xraw[g, u][:].rearrange("p (e n) -> p n e", e=2)
                cut = XG_LAST if (g, u) == (PASSES - 1, 1) else XG
                nc.scalar.copy(out=pair[:, cut:, :], in_=src[:, cut:, :])
                nc.gpsimd.tensor_scalar(pair[:, :cut, :], src[:, :cut, :], 1.0, 0.0, MULT, ADD)
                words = pair[:].rearrange("p n e -> p (n e)").bitcast(U32)
                nc.vector.tensor_copy(out=xg_words[:, :, u], in_=words.indirect(offsets[:]))
            xcodes[g] = keep.tile([P, SLOTS], U32, name="xcodes%d" % g, align_bytes=64)
            xscales[g] = keep.tile([P, SLOTS], U8, name="xscales%d" % g, align_bytes=64)
            nc.vector.quantize_mx(out=xcodes[g][:].bitcast(FP8X4), scales=xscales[g][:], in_=xg[:])

        weights = {}

        def prepare(e, g, name):
            wb = keep.tile([P, N, 4], BF16, name=name, align_bytes=64)
            parts = MT if (e, g) in BY_TILE else 1
            width = N // parts
            for i in range(parts):
                lo, hi = i * width, (i + 1) * width
                raw, base = wraw[e, g, lo // P]
                mid = lo + WG.get((e, g), 0) // parts
                nc.scalar.copy(
                    out=wb[:, mid:hi, :].rearrange("p (c i) j -> p c j i", i=4),
                    in_=raw[:, :, mid - base : hi - base].rearrange("p j (c i) -> p c j i", i=4),
                )
                if mid > lo:
                    src = raw[:, :, lo - base : mid - base].rearrange("p j n -> p n j")
                    nc.gpsimd.tensor_scalar(wb[:, lo:mid, :], src, 1.0, 0.0, MULT, ADD)
                codes = keep.tile([P, width], U32, name="wcodes%d%d%d" % (e, g, i), align_bytes=64)
                scales = keep.tile([P, width], U8, name="wscales%d%d%d" % (e, g, i), align_bytes=64)
                nc.vector.quantize_mx(
                    out=codes[:].bitcast(FP8X4),
                    scales=scales[:],
                    in_=wb[:, lo:hi, :].rearrange("p n j -> p (n j)"),
                )
                for m in range(lo // P, hi // P):
                    cols = slice(m * P - lo, (m + 1) * P - lo)
                    weights[e, g, m] = (codes[:, cols].bitcast(FP8X4), scales[:, cols])

        def put_back(e, m, name):
            acc = psum.tile([P, C], F32, name="acc0" if e == 0 else "acc1%d" % m)
            for g in range(PASSES):
                codes, scales = weights[e, g, m]
                nc.tensor.matmul_mx(
                    out=acc[:],
                    lhsT=codes,
                    lhsT_scale=scales,
                    rhs=xcodes[g][:, e * C : (e + 1) * C].bitcast(FP8X4),
                    rhs_scale=xscales[g][:, e * C : (e + 1) * C],
                    start=(g == 0),
                    stop=(g == PASSES - 1),
                )
            y = keep.tile([P, C], F32, name=name, align_bytes=64)
            nc.scalar.copy(out=y[:], in_=acc[:])
            nc.vector.tensor_copy(
                out=window[m][:].indirect(offsets[:, e * (C // 16) : (e + 1) * (C // 16)]),
                in_=y[:],
            )
            if e == E - 1:
                nc.sync.dma_start(out=out[m * P : (m + 1) * P, :], in_=window[m][:])

        for g in range(PASSES):
            prepare(0, g, "wb0%d" % g)
        put_back(0, 0, "y00")
        for g in range(PASSES):
            prepare(1, g, "wb1%d" % g)
        put_back(0, 1, "wraw120")
        put_back(1, 0, "y10")
        put_back(1, 1, "y11")
